import numpy as np
import ml_dtypes


def mxq(x, axis, fmt="e4m3"):
    dtype, down = {"e4m3": (ml_dtypes.float8_e4m3fn, 7), "e5m2": (ml_dtypes.float8_e5m2, 14)}[fmt]
    v = np.moveaxis(np.asarray(x, np.float32).astype(ml_dtypes.bfloat16).astype(np.float64), axis, -1)
    blocks = v.reshape(v.shape[:-1] + (-1, 32))
    amax = np.abs(blocks).max(-1, keepdims=True)
    byte = np.maximum(np.where(amax > 0, np.frexp(amax)[1] - 1 + 127, 0) - down, 1)
    scale = np.exp2(byte - 127.0)
    codes = (blocks / scale).astype(np.float32).astype(dtype).astype(np.float64)
    return np.moveaxis((codes * scale).reshape(v.shape), -1, axis)


WIDE = False


def mx_kscale(k):
    if not WIDE:
        return np.ones(k)
    levels = np.array([10, -10, 5, -5, 0])
    if k % 512:
        return np.exp2(np.random.permutation(np.resize(levels, k // 32))).repeat(32)
    a = np.empty((k // 512, 16))
    for p in range(k // 512):
        a[p, :8] = np.random.permutation(np.resize(levels, 8))
        for g in range(8):
            far = levels[np.abs(levels - a[p, g]) >= 10]
            a[p, g + 8] = far[np.random.randint(len(far))]
    return np.exp2(a.ravel()).repeat(32)


def f64(x):
    return np.asarray(x).astype(np.float64)


def striped8(idx):
    return np.concatenate([v.reshape(-1, 16).T for v in idx]).astype(np.uint16)


def unstriped8(offs):
    return np.stack([offs[16 * g:16 * g + 16].T.reshape(-1) for g in range(8)]).astype(np.int64)


def split(x):
    m, e = np.frexp(f64(x))
    hi = np.ldexp(np.trunc(16.0 * m) / 16.0, e)
    return hi, f64(x) - hi


def silu(v):
    return v / (1.0 + np.exp(-np.maximum(v, -700.0)))


K, M, T, S = 1536, 256, 1024, 512


def setup_inputs():
    n = np.random.standard_normal
    s = mx_kscale(K)[:, None]
    return {
        "xT": (n((K, T)) * s).astype(np.float32),
        "w": (n((K, M)) / np.sqrt(K) / s).astype(np.float32),
        "wgt": np.repeat(np.random.uniform(0.5, 2.0, (8, S)), 16, axis=0).astype(np.float32),
        "b": (0.3 * n(256)).astype(np.float32),
        "offs": striped8(np.stack([np.random.permutation(T)[:S] for _ in range(8)])),
    }


def reference(xT, w, wgt, b, offs):
    idx = unstriped8(offs)
    group = np.arange(K) % 512 // 64
    xg = f64(wgt)[np.arange(K) // 4 % 128] * f64(xT)[np.arange(K)[:, None], idx[group]]
    xT_ = mxq(xg, 0, "e4m3")
    w_hi, w_lo = split(w)
    w_hi_, w_lo_ = mxq(w_hi, 0, "e4m3"), mxq(w_lo, 0, "e4m3")
    y = xT_.T @ w_hi_ + xT_.T @ w_lo_
    return silu(y + f64(b)[None, :])

@@ -1,0 +1,208 @@
+from contextlib import ExitStack
+
+import concourse.mybir as mybir
+
+K, N, TOKENS, PICKS = 1536, 256, 1024, 512
+FLOPS = 2 * 2 * K * N * PICKS
+
+F32 = mybir.dt.float32
+BF16 = mybir.dt.bfloat16
+I32 = mybir.dt.int32
+U32 = mybir.dt.uint32
+U16 = mybir.dt.uint16
+U8 = mybir.dt.uint8
+FP8X4 = mybir.dt.float8_e4m3fn_x4
+ACT = mybir.ActivationFunctionType
+ALU = mybir.AluOpType
+
+P = 128
+PACK = 4
+K_PASS = P * PACK
+PASSES = K // K_PASS
+ROW_TILES = PICKS // P
+
+KEEP_HIGH_BITS = -0x000F0010
+
+
+def tile_list_heads_tm_hl_silu_kernel(tc, xT, w, wgt, b, offs, out):
+    nc = tc.nc
+
+    with ExitStack() as ctx:
+        keep = ctx.enter_context(tc.tile_pool(name="keep", bufs=1))
+        psum = ctx.enter_context(tc.psum_pool(name="psum", bufs=1))
+
+        def held(shape, dtype, name):
+            return keep.tile(shape, dtype, name=name, align_bytes=64)
+
+        offsets = keep.tile([P, PICKS // 16], U16, name="offsets")
+        weights = [held([P, PICKS // 2], F32, f"weights{h}") for h in range(2)]
+        bias = held([P, N], F32, "bias")
+        warm = held([P, 1], F32, "warm")
+        planes = [[held([P, TOKENS], F32, f"plane{a}_{i}") for i in range(PACK)] for a in range(PASSES)]
+        w_raw = [held([P, PACK, N], F32, f"w_raw{a}") for a in range(PASSES)]
+        w_top = [held([P, N, PACK], BF16, f"w_top{a}") for a in range(PASSES)]
+        w_hl = [held([P, 2, N, PACK], BF16, f"w_hl{a}") for a in range(PASSES)]
+        w_codes = [held([P, 2, N], U32, f"w_codes{a}") for a in range(PASSES)]
+        w_scales = [held([P, 2, N], U8, f"w_scales{a}") for a in range(PASSES)]
+        grouped = [held([P, PICKS, PACK], BF16, f"grouped{a}") for a in range(PASSES)]
+        x_codes = [held([P, PICKS], U32, f"x_codes{a}") for a in range(PASSES)]
+        x_scales = [held([P, PICKS], U8, f"x_scales{a}") for a in range(PASSES)]
+        sums = [psum.tile([P, 512], F32, name=f"sums{t}") for t in range(ROW_TILES)]
+
+        def load_w(a):
+            nc.sync.dma_start(w_raw[a][:], w[a * K_PASS : (a + 1) * K_PASS, :].rearrange("(p i) n -> p i n", i=PACK))
+
+        def load_plane(a, i):
+            nc.sync.dma_start(
+                planes[a][i][:],
+                xT[a * K_PASS : (a + 1) * K_PASS, :].rearrange("(p i) t -> p i t", i=PACK)[:, i, :],
+            )
+
+        nc.vector.memset(warm[:], 0.0)
+        nc.scalar.activation(warm[:], warm[:], ACT.Silu)
+
+        def load_weights(h):
+            nc.sync.dma_start(weights[h][:], wgt[:, h * PICKS // 2 : (h + 1) * PICKS // 2])
+
+        nc.sync.dma_start(offsets[:], offs)
+        load_weights(0)
+        load_plane(0, 0)
+        load_weights(1)
+        load_plane(0, 1)
+        load_w(0)
+        load_plane(0, 2)
+        load_plane(0, 3)
+        for a in (1, 2):
+            load_plane(a, 0)
+            load_w(a)
+            for i in range(1, PACK):
+                load_plane(a, i)
+        nc.sync.dma_start(bias[:], b.partition_broadcast(P))
+
+        def mask_w(a):
+            halves = w_raw[a][:].bitcast(BF16)[:, :, 1 : 2 * N : 2]
+            nc.scalar.copy(w_top[a][:], halves.rearrange("p i n -> p n i"))
+            nc.vector.tensor_scalar(
+                w_hl[a][:, 0].rearrange("p n i -> p (n i)").bitcast(I32),
+                w_top[a][:].rearrange("p n i -> p (n i)").bitcast(I32),
+                KEEP_HIGH_BITS,
+                None,
+                ALU.bitwise_and,
+            )
+
+        def subtract_w(a):
+            nc.vector.tensor_tensor(
+                w_hl[a][:, 1], w_raw[a][:].rearrange("p i n -> p n i"), w_hl[a][:, 0], ALU.subtract
+            )
+
+        def quantize_w(a):
+            nc.vector.quantize_mx(
+                out=w_codes[a][:].rearrange("p h n -> p (h n)").bitcast(FP8X4),
+                scales=w_scales[a][:].rearrange("p h n -> p (h n)"),
+                in_=w_hl[a][:].rearrange("p h n i -> p (h n i)"),
+            )
+
+        cuts = [((0, 256), (256, 512)), ((0, 256), (256, 512)), ((0, 256), (256, 384), (384, 512))]
+        picked = [
+            {lo: held([P, PACK, hi - lo], F32, f"picked{a}_{lo}") for lo, hi in cuts[a]} for a in range(PASSES)
+        ]
+
+        def gather(a, i, c):
+            lo, hi = cuts[a][c]
+            h, first = divmod(lo, PICKS // 2)
+            nc.vector.tensor_tensor(
+                picked[a][lo][:, i, :],
+                planes[a][i][:].indirect(offsets[:, lo // 16 : hi // 16]),
+                weights[h][:, first : first + hi - lo],
+                ALU.mult,
+            )
+
+        def interleave(a, c):
+            lo, hi = cuts[a][c]
+            nc.scalar.copy(grouped[a][:, lo:hi, :], picked[a][lo][:].rearrange("p i j -> p j i"))
+
+        def quantize_x(a, lo, hi):
+            nc.vector.quantize_mx(
+                out=x_codes[a][:, lo:hi].bitcast(FP8X4),
+                scales=x_scales[a][:, lo:hi],
+                in_=grouped[a][:, lo:hi, :].rearrange("p j i -> p (j i)"),
+            )
+
+        def multiply(a, t):
+            rows = slice(t * P, (t + 1) * P)
+            for h in range(2):
+                nc.tensor.matmul_mx(
+                    out=sums[t][:, 0:N],
+                    lhsT=x_codes[a][:, rows].bitcast(FP8X4),
+                    lhsT_scale=x_scales[a][:, rows],
+                    rhs=w_codes[a][:, h, :].bitcast(FP8X4),
+                    rhs_scale=w_scales[a][:, h, :],
+                    start=(a == 0 and h == 0),
+                    stop=(a == PASSES - 1 and h == 1),
+                )
+
+        def finish(t):
+            shifted = keep.tile([P, N], F32, name=f"shifted{t}")
+            nc.vector.tensor_tensor(shifted[:], sums[t][:, 0:N], bias[:], ALU.add)
+            result = keep.tile([P, N], F32, name=f"result{t}")
+            nc.scalar.activation(result[:], shifted[:], ACT.Silu)
+            nc.sync.dma_start(out[t * P : (t + 1) * P, :], result[:])
+
+        def multiply_all(a):
+            for t in range(ROW_TILES):
+                multiply(a, t)
+
+        for i in range(PACK):
+            gather(0, i, 0)
+            gather(0, i, 1)
+            if i == 1:
+                mask_w(0)
+            if i == 2:
+                subtract_w(0)
+        interleave(0, 0)
+        interleave(0, 1)
+        quantize_w(0)
+
+        for i in range(PACK):
+            gather(1, i, 0)
+            gather(1, i, 1)
+            if i == 0:
+                mask_w(1)
+            if i == 1:
+                subtract_w(1)
+            if i == 2:
+                quantize_x(0, 0, 512)
+                multiply_all(0)
+                quantize_w(1)
+        interleave(1, 0)
+        interleave(1, 1)
+
+        for i in range(PACK):
+            gather(2, i, 0)
+            if i == 0:
+                mask_w(2)
+            if i == 1:
+                subtract_w(2)
+        interleave(2, 0)
+        for i in range(PACK):
+            gather(2, i, 1)
+            if i == 0:
+                quantize_x(1, 0, 512)
+                multiply_all(1)
+            if i == 1:
+                quantize_w(2)
+        interleave(2, 1)
+        for i in range(PACK):
+            gather(2, i, 2)
+            if i == 1:
+                quantize_x(2, 0, 256)
+                multiply(2, 0)
+                multiply(2, 1)
+        interleave(2, 2)
+        quantize_x(2, 256, 384)
+        multiply(2, 2)
+        for t in range(3):
+            finish(t)
+        quantize_x(2, 384, 512)
+        multiply(2, 3)
+        finish(3)

@@ -35,18 +35,15 @@ def tile_list_heads_tm_hl_silu_kernel(tc, xT, w, wgt, b, offs, out):
             return keep.tile(shape, dtype, name=name, align_bytes=64)
 
         offsets = keep.tile([P, PICKS // 16], U16, name="offsets")
-        weights = [held([P, PICKS // 2], F32, f"weights{h}") for h in range(2)]
+        weights = held([P, PICKS], F32, "weights")
         bias = held([P, N], F32, "bias")
         warm = held([P, 1], F32, "warm")
         planes = [[held([P, TOKENS], F32, f"plane{a}_{i}") for i in range(PACK)] for a in range(PASSES)]
         w_raw = [held([P, PACK, N], F32, f"w_raw{a}") for a in range(PASSES)]
         w_top = [held([P, N, PACK], BF16, f"w_top{a}") for a in range(PASSES)]
-        w_hl = [held([P, 2, N, PACK], BF16, f"w_hl{a}") for a in range(PASSES)]
-        w_codes = [held([P, 2, N], U32, f"w_codes{a}") for a in range(PASSES)]
-        w_scales = [held([P, 2, N], U8, f"w_scales{a}") for a in range(PASSES)]
-        grouped = [held([P, PICKS, PACK], BF16, f"grouped{a}") for a in range(PASSES)]
-        x_codes = [held([P, PICKS], U32, f"x_codes{a}") for a in range(PASSES)]
-        x_scales = [held([P, PICKS], U8, f"x_scales{a}") for a in range(PASSES)]
+        grouped = [held([P, PICKS + 2 * N, PACK], BF16, f"grouped{a}") for a in range(PASSES)]
+        codes = [held([P, PICKS + 2 * N], U32, f"codes{a}") for a in range(PASSES)]
+        scales = [held([P, PICKS + 2 * N], U8, f"scales{a}") for a in range(PASSES)]
         sums = [psum.tile([P, 512], F32, name=f"sums{t}") for t in range(ROW_TILES)]
 
         def load_w(a):
@@ -61,29 +58,39 @@ def tile_list_heads_tm_hl_silu_kernel(tc, xT, w, wgt, b, offs, out):
         nc.vector.memset(warm[:], 0.0)
         nc.scalar.activation(warm[:], warm[:], ACT.Silu)
 
-        def load_weights(h):
-            nc.sync.dma_start(weights[h][:], wgt[:, h * PICKS // 2 : (h + 1) * PICKS // 2])
-
         nc.sync.dma_start(offsets[:], offs)
-        load_weights(0)
+        half = PICKS // 2
+        nc.sync.dma_start(weights[:, 0:half], wgt[:, 0:half])
         load_plane(0, 0)
-        load_weights(1)
+        nc.sync.dma_start(weights[:, half:PICKS], wgt[:, half:PICKS])
         load_plane(0, 1)
         load_w(0)
         load_plane(0, 2)
         load_plane(0, 3)
-        for a in (1, 2):
-            load_plane(a, 0)
-            load_w(a)
-            for i in range(1, PACK):
-                load_plane(a, i)
+        load_plane(1, 0)
+        load_w(1)
+        load_plane(1, 1)
+        load_plane(1, 2)
+        load_plane(1, 3)
+        load_w(2)
+        for i in range(PACK):
+            load_plane(2, i)
         nc.sync.dma_start(bias[:], b.partition_broadcast(P))
 
+        HI, LO, END = PICKS, PICKS + N, PICKS + 2 * N
+
+        def by_rows(interleaved):
+            return interleaved.rearrange("p (c e) i -> p c i e", e=4)
+
+        def by_planes(separate):
+            return separate.rearrange("p i (c e) -> p c i e", e=4)
+
+        def truncate_w(a):
+            nc.scalar.copy(by_rows(w_top[a][:]), by_planes(w_raw[a][:].bitcast(BF16)[:, :, 1 : 2 * N : 2]))
+
         def mask_w(a):
-            halves = w_raw[a][:].bitcast(BF16)[:, :, 1 : 2 * N : 2]
-            nc.scalar.copy(w_top[a][:], halves.rearrange("p i n -> p n i"))
             nc.vector.tensor_scalar(
-                w_hl[a][:, 0].rearrange("p n i -> p (n i)").bitcast(I32),
+                grouped[a][:, HI:LO, :].rearrange("p n i -> p (n i)").bitcast(I32),
                 w_top[a][:].rearrange("p n i -> p (n i)").bitcast(I32),
                 KEEP_HIGH_BITS,
                 None,
@@ -92,51 +99,47 @@ def tile_list_heads_tm_hl_silu_kernel(tc, xT, w, wgt, b, offs, out):
 
         def subtract_w(a):
             nc.vector.tensor_tensor(
-                w_hl[a][:, 1], w_raw[a][:].rearrange("p i n -> p n i"), w_hl[a][:, 0], ALU.subtract
+                by_rows(grouped[a][:, LO:END, :]),
+                by_planes(w_raw[a][:]),
+                by_rows(grouped[a][:, HI:LO, :]),
+                ALU.subtract,
             )
 
-        def quantize_w(a):
-            nc.vector.quantize_mx(
-                out=w_codes[a][:].rearrange("p h n -> p (h n)").bitcast(FP8X4),
-                scales=w_scales[a][:].rearrange("p h n -> p (h n)"),
-                in_=w_hl[a][:].rearrange("p h n i -> p (h n i)"),
-            )
-
-        cuts = [((0, 256), (256, 512)), ((0, 256), (256, 512)), ((0, 256), (256, 384), (384, 512))]
+        cuts = [((0, 256), (256, 512)), ((0, 256), (256, 512)), ((0, 384), (384, 512))]
         picked = [
             {lo: held([P, PACK, hi - lo], F32, f"picked{a}_{lo}") for lo, hi in cuts[a]} for a in range(PASSES)
         ]
 
         def gather(a, i, c):
             lo, hi = cuts[a][c]
-            h, first = divmod(lo, PICKS // 2)
             nc.vector.tensor_tensor(
                 picked[a][lo][:, i, :],
                 planes[a][i][:].indirect(offsets[:, lo // 16 : hi // 16]),
-                weights[h][:, first : first + hi - lo],
+                weights[:, lo:hi],
                 ALU.mult,
             )
 
         def interleave(a, c):
             lo, hi = cuts[a][c]
-            nc.scalar.copy(grouped[a][:, lo:hi, :], picked[a][lo][:].rearrange("p i j -> p j i"))
+            nc.scalar.copy(by_rows(grouped[a][:, lo:hi, :]), by_planes(picked[a][lo][:]))
 
-        def quantize_x(a, lo, hi):
+        def quantize(a, lo, hi):
             nc.vector.quantize_mx(
-                out=x_codes[a][:, lo:hi].bitcast(FP8X4),
-                scales=x_scales[a][:, lo:hi],
+                out=codes[a][:, lo:hi].bitcast(FP8X4),
+                scales=scales[a][:, lo:hi],
                 in_=grouped[a][:, lo:hi, :].rearrange("p j i -> p (j i)"),
             )
 
         def multiply(a, t):
             rows = slice(t * P, (t + 1) * P)
             for h in range(2):
+                cols = slice(HI + h * N, LO + h * N)
                 nc.tensor.matmul_mx(
                     out=sums[t][:, 0:N],
-                    lhsT=x_codes[a][:, rows].bitcast(FP8X4),
-                    lhsT_scale=x_scales[a][:, rows],
-                    rhs=w_codes[a][:, h, :].bitcast(FP8X4),
-                    rhs_scale=w_scales[a][:, h, :],
+                    lhsT=codes[a][:, rows].bitcast(FP8X4),
+                    lhsT_scale=scales[a][:, rows],
+                    rhs=codes[a][:, cols].bitcast(FP8X4),
+                    rhs_scale=scales[a][:, cols],
                     start=(a == 0 and h == 0),
                     stop=(a == PASSES - 1 and h == 1),
                 )
@@ -152,57 +155,55 @@ def tile_list_heads_tm_hl_silu_kernel(tc, xT, w, wgt, b, offs, out):
             for t in range(ROW_TILES):
                 multiply(a, t)
 
-        for i in range(PACK):
-            gather(0, i, 0)
-            gather(0, i, 1)
-            if i == 1:
-                mask_w(0)
-            if i == 2:
-                subtract_w(0)
+        def gather_plane(a, i):
+            for c in range(2):
+                gather(a, i, c)
+
+        gather_plane(0, 0)
+        gather_plane(0, 1)
+        truncate_w(0)
+        mask_w(0)
+        gather_plane(0, 2)
+        subtract_w(0)
+        gather_plane(0, 3)
+        truncate_w(1)
         interleave(0, 0)
         interleave(0, 1)
-        quantize_w(0)
-
-        for i in range(PACK):
-            gather(1, i, 0)
-            gather(1, i, 1)
-            if i == 0:
-                mask_w(1)
-            if i == 1:
-                subtract_w(1)
-            if i == 2:
-                quantize_x(0, 0, 512)
-                multiply_all(0)
-                quantize_w(1)
+        gather_plane(1, 0)
+        mask_w(1)
+        gather_plane(1, 1)
+        subtract_w(1)
+        gather_plane(1, 2)
+        truncate_w(2)
+        quantize(0, 0, END)
+        multiply_all(0)
+        gather_plane(1, 3)
         interleave(1, 0)
         interleave(1, 1)
 
-        for i in range(PACK):
-            gather(2, i, 0)
-            if i == 0:
-                mask_w(2)
-            if i == 1:
-                subtract_w(2)
+        gather(2, 0, 0)
+        mask_w(2)
+        gather(2, 1, 0)
+        subtract_w(2)
+        gather(2, 2, 0)
+        gather(2, 3, 0)
         interleave(2, 0)
-        for i in range(PACK):
-            gather(2, i, 1)
-            if i == 0:
-                quantize_x(1, 0, 512)
-                multiply_all(1)
-            if i == 1:
-                quantize_w(2)
-        interleave(2, 1)
-        for i in range(PACK):
-            gather(2, i, 2)
-            if i == 1:
-                quantize_x(2, 0, 256)
-                multiply(2, 0)
-                multiply(2, 1)
-        interleave(2, 2)
-        quantize_x(2, 256, 384)
+        quantize(1, 0, END)
+        multiply_all(1)
+        gather(2, 0, 1)
+        quantize(2, HI, END)
+        gather(2, 1, 1)
+        gather(2, 2, 1)
+        quantize(2, 0, 256)
+        multiply(2, 0)
+        multiply(2, 1)
+        quantize(2, 256, 384)
         multiply(2, 2)
-        for t in range(3):
-            finish(t)
-        quantize_x(2, 384, 512)
+        gather(2, 3, 1)
+        interleave(2, 1)
+        finish(0)
+        finish(1)
+        quantize(2, 384, 512)
         multiply(2, 3)
+        finish(2)
         finish(3)

@@ -63,13 +63,12 @@ def tile_list_heads_tm_hl_silu_kernel(tc, xT, w, wgt, b, offs, out):
         nc.sync.dma_start(weights[:, 0:half], wgt[:, 0:half])
         load_plane(0, 0)
         nc.sync.dma_start(weights[:, half:PICKS], wgt[:, half:PICKS])
-        load_plane(0, 1)
+        for i in range(1, PACK):
+            load_plane(0, i)
         load_w(0)
-        load_plane(0, 2)
-        load_plane(0, 3)
         load_plane(1, 0)
-        load_w(1)
         load_plane(1, 1)
+        load_w(1)
         load_plane(1, 2)
         load_plane(1, 3)
         load_w(2)
@@ -123,6 +122,13 @@ def tile_list_heads_tm_hl_silu_kernel(tc, xT, w, wgt, b, offs, out):
             lo, hi = cuts[a][c]
             nc.scalar.copy(by_rows(grouped[a][:, lo:hi, :]), by_planes(picked[a][lo][:]))
 
+        def interleave_last():
+            lo, hi = cuts[2][1]
+            mid = 448
+            source = picked[2][lo]
+            nc.scalar.copy(by_rows(grouped[2][:, mid:hi, :]), by_planes(source[:, :, mid - lo : hi - lo]))
+            nc.vector.tensor_copy(by_rows(grouped[2][:, lo:mid, :]), by_planes(source[:, :, 0 : mid - lo]))
+
         def quantize(a, lo, hi):
             nc.vector.quantize_mx(
                 out=codes[a][:, lo:hi].bitcast(FP8X4),
@@ -159,25 +165,23 @@ def tile_list_heads_tm_hl_silu_kernel(tc, xT, w, wgt, b, offs, out):
             for c in range(2):
                 gather(a, i, c)
 
-        gather_plane(0, 0)
-        gather_plane(0, 1)
+        for i in range(PACK):
+            gather_plane(0, i)
         truncate_w(0)
-        mask_w(0)
-        gather_plane(0, 2)
-        subtract_w(0)
-        gather_plane(0, 3)
-        truncate_w(1)
         interleave(0, 0)
         interleave(0, 1)
         gather_plane(1, 0)
-        mask_w(1)
+        mask_w(0)
         gather_plane(1, 1)
-        subtract_w(1)
+        subtract_w(0)
+        truncate_w(1)
         gather_plane(1, 2)
-        truncate_w(2)
+        mask_w(1)
         quantize(0, 0, END)
         multiply_all(0)
         gather_plane(1, 3)
+        subtract_w(1)
+        truncate_w(2)
         interleave(1, 0)
         interleave(1, 1)
 
@@ -200,8 +204,8 @@ def tile_list_heads_tm_hl_silu_kernel(tc, xT, w, wgt, b, offs, out):
         quantize(2, 256, 384)
         multiply(2, 2)
         gather(2, 3, 1)
-        interleave(2, 1)
         finish(0)
+        interleave_last()
         finish(1)
         quantize(2, 384, 512)
         multiply(2, 3)

from contextlib import ExitStack

import concourse.mybir as mybir

K, N, TOKENS, PICKS = 1536, 256, 1024, 512
FLOPS = 2 * 2 * K * N * PICKS

F32 = mybir.dt.float32
BF16 = mybir.dt.bfloat16
I32 = mybir.dt.int32
U32 = mybir.dt.uint32
U16 = mybir.dt.uint16
U8 = mybir.dt.uint8
FP8X4 = mybir.dt.float8_e4m3fn_x4
ACT = mybir.ActivationFunctionType
ALU = mybir.AluOpType

P = 128
PACK = 4
K_PASS = P * PACK
PASSES = K // K_PASS
ROW_TILES = PICKS // P

KEEP_HIGH_BITS = -0x000F0010


def tile_list_heads_tm_hl_silu_kernel(tc, xT, w, wgt, b, offs, out):
    nc = tc.nc

    with ExitStack() as ctx:
        keep = ctx.enter_context(tc.tile_pool(name="keep", bufs=1))
        psum = ctx.enter_context(tc.psum_pool(name="psum", bufs=1))

        def held(shape, dtype, name):
            return keep.tile(shape, dtype, name=name, align_bytes=64)

        offsets = keep.tile([P, PICKS // 16], U16, name="offsets")
        weights = held([P, PICKS], F32, "weights")
        bias = held([P, N], F32, "bias")
        warm = held([P, 1], F32, "warm")
        planes = [[held([P, TOKENS], F32, f"plane{a}_{i}") for i in range(PACK)] for a in range(PASSES)]
        w_raw = [held([P, PACK, N], F32, f"w_raw{a}") for a in range(PASSES)]
        w_top = [held([P, N, PACK], BF16, f"w_top{a}") for a in range(PASSES)]
        grouped = [held([P, PICKS + 2 * N, PACK], BF16, f"grouped{a}") for a in range(PASSES)]
        codes = [held([P, PICKS + 2 * N], U32, f"codes{a}") for a in range(PASSES)]
        scales = [held([P, PICKS + 2 * N], U8, f"scales{a}") for a in range(PASSES)]
        sums = [psum.tile([P, 512], F32, name=f"sums{t}") for t in range(ROW_TILES)]

        def load_w(a):
            nc.sync.dma_start(w_raw[a][:], w[a * K_PASS : (a + 1) * K_PASS, :].rearrange("(p i) n -> p i n", i=PACK))

        def load_plane(a, i):
            nc.sync.dma_start(
                planes[a][i][:],
                xT[a * K_PASS : (a + 1) * K_PASS, :].rearrange("(p i) t -> p i t", i=PACK)[:, i, :],
            )

        nc.vector.memset(warm[:], 0.0)
        nc.scalar.activation(warm[:], warm[:], ACT.Silu)

        nc.sync.dma_start(offsets[:], offs)
        half = PICKS // 2
        nc.sync.dma_start(weights[:, 0:half], wgt[:, 0:half])
        load_plane(0, 0)
        nc.sync.dma_start(weights[:, half:PICKS], wgt[:, half:PICKS])
        for i in range(1, PACK):
            load_plane(0, i)
        load_w(0)
        load_plane(1, 0)
        load_plane(1, 1)
        load_w(1)
        load_plane(1, 2)
        load_plane(1, 3)
        load_w(2)
        for i in range(PACK):
            load_plane(2, i)
        nc.sync.dma_start(bias[:], b.partition_broadcast(P))

        HI, LO, END = PICKS, PICKS + N, PICKS + 2 * N

        def by_rows(interleaved):
            return interleaved.rearrange("p (c e) i -> p c i e", e=4)

        def by_planes(separate):
            return separate.rearrange("p i (c e) -> p c i e", e=4)

        def truncate_w(a):
            nc.scalar.copy(by_rows(w_top[a][:]), by_planes(w_raw[a][:].bitcast(BF16)[:, :, 1 : 2 * N : 2]))

        def mask_w(a):
            nc.vector.tensor_scalar(
                grouped[a][:, HI:LO, :].rearrange("p n i -> p (n i)").bitcast(I32),
                w_top[a][:].rearrange("p n i -> p (n i)").bitcast(I32),
                KEEP_HIGH_BITS,
                None,
                ALU.bitwise_and,
            )

        def subtract_w(a):
            nc.vector.tensor_tensor(
                by_rows(grouped[a][:, LO:END, :]),
                by_planes(w_raw[a][:]),
                by_rows(grouped[a][:, HI:LO, :]),
                ALU.subtract,
            )

        cuts = [((0, 256), (256, 512)), ((0, 256), (256, 512)), ((0, 384), (384, 512))]
        picked = [
            {lo: held([P, PACK, hi - lo], F32, f"picked{a}_{lo}") for lo, hi in cuts[a]} for a in range(PASSES)
        ]

        def gather(a, i, c):
            lo, hi = cuts[a][c]
            nc.vector.tensor_tensor(
                picked[a][lo][:, i, :],
                planes[a][i][:].indirect(offsets[:, lo // 16 : hi // 16]),
                weights[:, lo:hi],
                ALU.mult,
            )

        def interleave(a, c):
            lo, hi = cuts[a][c]
            nc.scalar.copy(by_rows(grouped[a][:, lo:hi, :]), by_planes(picked[a][lo][:]))

        def interleave_last():
            lo, hi = cuts[2][1]
            mid = 448
            source = picked[2][lo]
            nc.scalar.copy(by_rows(grouped[2][:, mid:hi, :]), by_planes(source[:, :, mid - lo : hi - lo]))
            nc.vector.tensor_copy(by_rows(grouped[2][:, lo:mid, :]), by_planes(source[:, :, 0 : mid - lo]))

        def quantize(a, lo, hi):
            nc.vector.quantize_mx(
                out=codes[a][:, lo:hi].bitcast(FP8X4),
                scales=scales[a][:, lo:hi],
                in_=grouped[a][:, lo:hi, :].rearrange("p j i -> p (j i)"),
            )

        def multiply(a, t):
            rows = slice(t * P, (t + 1) * P)
            for h in range(2):
                cols = slice(HI + h * N, LO + h * N)
                nc.tensor.matmul_mx(
                    out=sums[t][:, 0:N],
                    lhsT=codes[a][:, rows].bitcast(FP8X4),
                    lhsT_scale=scales[a][:, rows],
                    rhs=codes[a][:, cols].bitcast(FP8X4),
                    rhs_scale=scales[a][:, cols],
                    start=(a == 0 and h == 0),
                    stop=(a == PASSES - 1 and h == 1),
                )

        def finish(t):
            shifted = keep.tile([P, N], F32, name=f"shifted{t}")
            nc.vector.tensor_tensor(shifted[:], sums[t][:, 0:N], bias[:], ALU.add)
            result = keep.tile([P, N], F32, name=f"result{t}")
            nc.scalar.activation(result[:], shifted[:], ACT.Silu)
            nc.sync.dma_start(out[t * P : (t + 1) * P, :], result[:])

        def multiply_all(a):
            for t in range(ROW_TILES):
                multiply(a, t)

        def gather_plane(a, i):
            for c in range(2):
                gather(a, i, c)

        for i in range(PACK):
            gather_plane(0, i)
        truncate_w(0)
        interleave(0, 0)
        interleave(0, 1)
        gather_plane(1, 0)
        mask_w(0)
        gather_plane(1, 1)
        subtract_w(0)
        truncate_w(1)
        gather_plane(1, 2)
        mask_w(1)
        quantize(0, 0, END)
        multiply_all(0)
        gather_plane(1, 3)
        subtract_w(1)
        truncate_w(2)
        interleave(1, 0)
        interleave(1, 1)

        gather(2, 0, 0)
        mask_w(2)
        gather(2, 1, 0)
        subtract_w(2)
        gather(2, 2, 0)
        gather(2, 3, 0)
        interleave(2, 0)
        quantize(1, 0, END)
        multiply_all(1)
        gather(2, 0, 1)
        quantize(2, HI, END)
        gather(2, 1, 1)
        gather(2, 2, 1)
        quantize(2, 0, 256)
        multiply(2, 0)
        multiply(2, 1)
        quantize(2, 256, 384)
        multiply(2, 2)
        gather(2, 3, 1)
        finish(0)
        interleave_last()
        finish(1)
        quantize(2, 384, 512)
        multiply(2, 3)
        finish(2)
        finish(3)
